import numpy as np
import ml_dtypes


def mxq(x, axis, fmt="e4m3"):
    dtype, down = {"e4m3": (ml_dtypes.float8_e4m3fn, 7), "e5m2": (ml_dtypes.float8_e5m2, 14)}[fmt]
    v = np.moveaxis(np.asarray(x, np.float32).astype(ml_dtypes.bfloat16).astype(np.float64), axis, -1)
    blocks = v.reshape(v.shape[:-1] + (-1, 32))
    amax = np.abs(blocks).max(-1, keepdims=True)
    byte = np.maximum(np.where(amax > 0, np.frexp(amax)[1] - 1 + 127, 0) - down, 1)
    scale = np.exp2(byte - 127.0)
    codes = (blocks / scale).astype(np.float32).astype(dtype).astype(np.float64)
    return np.moveaxis((codes * scale).reshape(v.shape), -1, axis)


WIDE = False


def mx_kscale(k):
    if not WIDE:
        return np.ones(k)
    levels = np.array([10, -10, 5, -5, 0])
    if k % 512:
        return np.exp2(np.random.permutation(np.resize(levels, k // 32))).repeat(32)
    a = np.empty((k // 512, 16))
    for p in range(k // 512):
        a[p, :8] = np.random.permutation(np.resize(levels, 8))
        for g in range(8):
            far = levels[np.abs(levels - a[p, g]) >= 10]
            a[p, g + 8] = far[np.random.randint(len(far))]
    return np.exp2(a.ravel()).repeat(32)


def f64(x):
    return np.asarray(x).astype(np.float64)


def striped(idx):
    return np.tile(idx.reshape(-1, 16).T, (8, 1)).astype(np.uint16)


def unstriped(offs):
    return offs[:16].T.reshape(-1).astype(np.int64)


K, T, D, S, V, N = 512, 4096, 2, 1024, 512, 256


def setup_inputs():
    n = np.random.standard_normal
    s = mx_kscale(K)[:, None]
    return {
        "xT": (n((K, T)) * s).astype(np.float32),
        "w": (n((D, K, N)) / np.sqrt(K) / s[None]).astype(np.float32),
        "offs": striped(np.random.permutation(T)[:S]),
    }


def reference(xT, w, offs):
    idx = unstriped(offs)
    xq = mxq(f64(xT)[:, idx], 0, "e4m3")
    wq = mxq(f64(w), 1, "e4m3")
    y0 = wq[0].T @ xq[:, :V]
    y1 = wq[1].T @ xq[:, V:]
    return y0 * y1

@@ -1,0 +1,85 @@
+import concourse.mybir as mybir
+
+K, T, S, V, N = 512, 4096, 1024, 512, 256
+P = 128
+PACK = 4
+M_TILES = N // P
+PIECE = 256
+
+FLOPS = 2 * K * N * S
+
+F32 = mybir.dt.float32
+BF16 = mybir.dt.bfloat16
+U32 = mybir.dt.uint32
+U16 = mybir.dt.uint16
+U8 = mybir.dt.uint8
+FP8X4 = mybir.dt.float8_e4m3fn_x4
+MULT = mybir.AluOpType.mult
+
+
+def tile_picked_pair_lin_mul_sub_e_kernel(tc, xT, w, offs, out):
+    nc = tc.nc
+    with (
+        tc.tile_pool(name="keep", bufs=1) as keep,
+        tc.psum_pool(name="psum", bufs=1) as psum,
+    ):
+        offsets = keep.tile([P, S // 16], U16, name="offsets")
+        nc.sync.dma_start(offsets[:], offs)
+
+        w_raw = keep.tile([P, 2, PACK, N], F32, name="w_raw")
+        for d in range(2):
+            nc.sync.dma_start(out=w_raw[:, d, :, :], in_=w[d].rearrange("(p j) n -> p j n", j=PACK))
+
+        x_rows = xT.rearrange("(p j) t -> p j t", j=PACK)
+        planes = []
+        for j in range(PACK):
+            plane = keep.tile([P, T], F32, name=f"plane{j}")
+            nc.sync.dma_start(out=plane[:], in_=x_rows[:, j, :])
+            planes.append(plane)
+
+        w_grouped = keep.tile([P, 2, N, PACK], BF16, name="w_grouped", align_bytes=64)
+        w_codes = keep.tile([P, 2 * N], U32, name="w_codes", align_bytes=64)
+        w_scales = keep.tile([P, 2 * N], U8, name="w_scales", align_bytes=64)
+        for d in range(2):
+            nc.scalar.copy(out=w_grouped[:, d, :, :], in_=w_raw[:, d, :, :].rearrange("p j n -> p n j"))
+        nc.vector.quantize_mx(
+            out=w_codes[:].bitcast(FP8X4),
+            scales=w_scales[:],
+            in_=w_grouped[:].rearrange("p d n j -> p (d n j)"),
+        )
+
+        x_grouped = [keep.tile([P, V, PACK], BF16, name=f"x_grouped{d}", align_bytes=64) for d in range(2)]
+        x_codes = [keep.tile([P, V], U32, name=f"x_codes{d}", align_bytes=64) for d in range(2)]
+        x_scales = [keep.tile([P, V], U8, name=f"x_scales{d}", align_bytes=64) for d in range(2)]
+        for j in range(PACK):
+            for d in range(2):
+                picked = planes[j][:].indirect(offsets[:, d * (V // 16) : (d + 1) * (V // 16)])
+                nc.vector.tensor_copy(x_grouped[d][:, :, j], picked)
+
+        for i in range(V // PIECE):
+            cols = slice(i * PIECE, (i + 1) * PIECE)
+            banks = []
+            for d in range(2):
+                nc.vector.quantize_mx(
+                    out=x_codes[d][:, cols].bitcast(FP8X4),
+                    scales=x_scales[d][:, cols],
+                    in_=x_grouped[d][:, cols, :].rearrange("p v j -> p (v j)"),
+                )
+                bank = psum.tile([P, M_TILES, PIECE], F32, name=f"y{d}_{i}")
+                for m in range(M_TILES):
+                    m_cols = slice(d * N + m * P, d * N + (m + 1) * P)
+                    nc.tensor.matmul_mx(
+                        out=bank[:, m, :],
+                        lhsT=w_codes[:, m_cols].bitcast(FP8X4),
+                        lhsT_scale=w_scales[:, m_cols],
+                        rhs=x_codes[d][:, cols].bitcast(FP8X4),
+                        rhs_scale=x_scales[d][:, cols],
+                        start=True,
+                        stop=True,
+                    )
+                banks.append(bank)
+            y0 = keep.tile([P, M_TILES, PIECE], F32, name=f"y0_sb{i}")
+            nc.scalar.copy(out=y0[:], in_=banks[0][:])
+            product = keep.tile([P, M_TILES, PIECE], F32, name=f"product{i}")
+            nc.vector.tensor_tensor(product[:], banks[1][:], y0[:], MULT)
+            nc.sync.dma_start(out=out[:, cols].rearrange("(m p) v -> p m v", p=P), in_=product[:])

@@ -4,7 +4,7 @@ K, T, S, V, N = 512, 4096, 1024, 512, 256
 P = 128
 PACK = 4
 M_TILES = N // P
-PIECE = 256
+LAST_PIECES = (256, 128, 128)
 
 FLOPS = 2 * K * N * S
 
@@ -51,35 +51,53 @@ def tile_picked_pair_lin_mul_sub_e_kernel(tc, xT, w, offs, out):
         x_grouped = [keep.tile([P, V, PACK], BF16, name=f"x_grouped{d}", align_bytes=64) for d in range(2)]
         x_codes = [keep.tile([P, V], U32, name=f"x_codes{d}", align_bytes=64) for d in range(2)]
         x_scales = [keep.tile([P, V], U8, name=f"x_scales{d}", align_bytes=64) for d in range(2)]
-        for j in range(PACK):
-            for d in range(2):
-                picked = planes[j][:].indirect(offsets[:, d * (V // 16) : (d + 1) * (V // 16)])
-                nc.vector.tensor_copy(x_grouped[d][:, :, j], picked)
+        y0 = keep.tile([P, M_TILES, V], F32, name="y0")
 
-        for i in range(V // PIECE):
-            cols = slice(i * PIECE, (i + 1) * PIECE)
-            banks = []
+        def gather(j, d):
+            picked = planes[j][:].indirect(offsets[:, d * (V // 16) : (d + 1) * (V // 16)])
+            nc.vector.tensor_copy(x_grouped[d][:, :, j], picked)
+
+        def quantise(d, cols):
+            nc.vector.quantize_mx(
+                out=x_codes[d][:, cols].bitcast(FP8X4),
+                scales=x_scales[d][:, cols],
+                in_=x_grouped[d][:, cols, :].rearrange("p v j -> p (v j)"),
+            )
+
+        def multiply(d, m, cols, acc):
+            m_cols = slice(d * N + m * P, d * N + (m + 1) * P)
+            nc.tensor.matmul_mx(
+                out=acc,
+                lhsT=w_codes[:, m_cols].bitcast(FP8X4),
+                lhsT_scale=w_scales[:, m_cols],
+                rhs=x_codes[d][:, cols].bitcast(FP8X4),
+                rhs_scale=x_scales[d][:, cols],
+                start=True,
+                stop=True,
+            )
+
+        for j in range(PACK - 1):
             for d in range(2):
-                nc.vector.quantize_mx(
-                    out=x_codes[d][:, cols].bitcast(FP8X4),
-                    scales=x_scales[d][:, cols],
-                    in_=x_grouped[d][:, cols, :].rearrange("p v j -> p (v j)"),
-                )
-                bank = psum.tile([P, M_TILES, PIECE], F32, name=f"y{d}_{i}")
-                for m in range(M_TILES):
-                    m_cols = slice(d * N + m * P, d * N + (m + 1) * P)
-                    nc.tensor.matmul_mx(
-                        out=bank[:, m, :],
-                        lhsT=w_codes[:, m_cols].bitcast(FP8X4),
-                        lhsT_scale=w_scales[:, m_cols],
-                        rhs=x_codes[d][:, cols].bitcast(FP8X4),
-                        rhs_scale=x_scales[d][:, cols],
-                        start=True,
-                        stop=True,
-                    )
-                banks.append(bank)
-            y0 = keep.tile([P, M_TILES, PIECE], F32, name=f"y0_sb{i}")
-            nc.scalar.copy(out=y0[:], in_=banks[0][:])
-            product = keep.tile([P, M_TILES, PIECE], F32, name=f"product{i}")
-            nc.vector.tensor_tensor(product[:], banks[1][:], y0[:], MULT)
-            nc.sync.dma_start(out=out[:, cols].rearrange("(m p) v -> p m v", p=P), in_=product[:])
+                gather(j, d)
+
+        every = slice(0, V)
+        gather(PACK - 1, 0)
+        quantise(0, every)
+        for m in range(M_TILES):
+            bank = psum.tile([P, V], F32, name=f"y0_{m}")
+            multiply(0, m, every, bank[:])
+            nc.scalar.copy(out=y0[:, m, :], in_=bank[:])
+
+        gather(PACK - 1, 1)
+        start = 0
+        for i, width in enumerate(LAST_PIECES):
+            cols = slice(start, start + width)
+            quantise(1, cols)
+            bank = psum.tile([P, M_TILES, width], F32, name=f"y1_{i}")
+            for m in range(M_TILES):
+                multiply(1, m, cols, bank[:, m, :])
+            product = keep.tile([P, M_TILES, width], F32, name=f"product{i}")
+            nc.vector.tensor_tensor(product[:], bank[:], y0[:, :, cols], MULT)
+            queue = nc.scalar if i == 1 else nc.sync
+            queue.dma_start(out=out[:, cols].rearrange("(m p) v -> p m v", p=P), in_=product[:])
+            start += width

@@ -4,7 +4,7 @@ K, T, S, V, N = 512, 4096, 1024, 512, 256
 P = 128
 PACK = 4
 M_TILES = N // P
-LAST_PIECES = (256, 128, 128)
+PIECE = 256
 
 FLOPS = 2 * K * N * S
 
@@ -26,10 +26,6 @@ def tile_picked_pair_lin_mul_sub_e_kernel(tc, xT, w, offs, out):
         offsets = keep.tile([P, S // 16], U16, name="offsets")
         nc.sync.dma_start(offsets[:], offs)
 
-        w_raw = keep.tile([P, 2, PACK, N], F32, name="w_raw")
-        for d in range(2):
-            nc.sync.dma_start(out=w_raw[:, d, :, :], in_=w[d].rearrange("(p j) n -> p j n", j=PACK))
-
         x_rows = xT.rearrange("(p j) t -> p j t", j=PACK)
         planes = []
         for j in range(PACK):
@@ -37,25 +33,30 @@ def tile_picked_pair_lin_mul_sub_e_kernel(tc, xT, w, offs, out):
             nc.sync.dma_start(out=plane[:], in_=x_rows[:, j, :])
             planes.append(plane)
 
-        w_grouped = keep.tile([P, 2, N, PACK], BF16, name="w_grouped", align_bytes=64)
-        w_codes = keep.tile([P, 2 * N], U32, name="w_codes", align_bytes=64)
-        w_scales = keep.tile([P, 2 * N], U8, name="w_scales", align_bytes=64)
+        w_raw = []
         for d in range(2):
-            nc.scalar.copy(out=w_grouped[:, d, :, :], in_=w_raw[:, d, :, :].rearrange("p j n -> p n j"))
-        nc.vector.quantize_mx(
-            out=w_codes[:].bitcast(FP8X4),
-            scales=w_scales[:],
-            in_=w_grouped[:].rearrange("p d n j -> p (d n j)"),
-        )
+            raw = keep.tile([P, PACK, N], F32, name=f"w_raw{d}")
+            nc.sync.dma_start(out=raw[:], in_=w[d].rearrange("(p j) n -> p j n", j=PACK))
+            w_raw.append(raw)
 
         x_grouped = [keep.tile([P, V, PACK], BF16, name=f"x_grouped{d}", align_bytes=64) for d in range(2)]
         x_codes = [keep.tile([P, V], U32, name=f"x_codes{d}", align_bytes=64) for d in range(2)]
         x_scales = [keep.tile([P, V], U8, name=f"x_scales{d}", align_bytes=64) for d in range(2)]
-        y0 = keep.tile([P, M_TILES, V], F32, name="y0")
+        for j in range(PACK):
+            for d in range(2):
+                picked = planes[j][:].indirect(offsets[:, d * (V // 16) : (d + 1) * (V // 16)])
+                nc.vector.tensor_copy(x_grouped[d][:, :, j], picked)
 
-        def gather(j, d):
-            picked = planes[j][:].indirect(offsets[:, d * (V // 16) : (d + 1) * (V // 16)])
-            nc.vector.tensor_copy(x_grouped[d][:, :, j], picked)
+        w_codes = [keep.tile([P, N], U32, name=f"w_codes{d}", align_bytes=64) for d in range(2)]
+        w_scales = [keep.tile([P, N], U8, name=f"w_scales{d}", align_bytes=64) for d in range(2)]
+        for d in range(2):
+            w_grouped = keep.tile([P, N, PACK], BF16, name=f"w_grouped{d}", align_bytes=64)
+            nc.scalar.copy(out=w_grouped[:], in_=w_raw[d][:].rearrange("p j n -> p n j"))
+            nc.vector.quantize_mx(
+                out=w_codes[d][:].bitcast(FP8X4),
+                scales=w_scales[d][:],
+                in_=w_grouped[:].rearrange("p n j -> p (n j)"),
+            )
 
         def quantise(d, cols):
             nc.vector.quantize_mx(
@@ -64,40 +65,41 @@ def tile_picked_pair_lin_mul_sub_e_kernel(tc, xT, w, offs, out):
                 in_=x_grouped[d][:, cols, :].rearrange("p v j -> p (v j)"),
             )
 
-        def multiply(d, m, cols, acc):
-            m_cols = slice(d * N + m * P, d * N + (m + 1) * P)
+        def product(d, m, cols, acc):
+            m_cols = slice(m * P, (m + 1) * P)
             nc.tensor.matmul_mx(
                 out=acc,
-                lhsT=w_codes[:, m_cols].bitcast(FP8X4),
-                lhsT_scale=w_scales[:, m_cols],
+                lhsT=w_codes[d][:, m_cols].bitcast(FP8X4),
+                lhsT_scale=w_scales[d][:, m_cols],
                 rhs=x_codes[d][:, cols].bitcast(FP8X4),
                 rhs_scale=x_scales[d][:, cols],
                 start=True,
                 stop=True,
             )
 
-        for j in range(PACK - 1):
+        first = slice(0, PIECE)
+        last = slice(PIECE, 2 * PIECE)
+        for cols in (first, last):
             for d in range(2):
-                gather(j, d)
+                quantise(d, cols)
 
-        every = slice(0, V)
-        gather(PACK - 1, 0)
-        quantise(0, every)
-        for m in range(M_TILES):
-            bank = psum.tile([P, V], F32, name=f"y0_{m}")
-            multiply(0, m, every, bank[:])
-            nc.scalar.copy(out=y0[:, m, :], in_=bank[:])
-
-        gather(PACK - 1, 1)
-        start = 0
-        for i, width in enumerate(LAST_PIECES):
-            cols = slice(start, start + width)
-            quantise(1, cols)
-            bank = psum.tile([P, M_TILES, width], F32, name=f"y1_{i}")
+        banks = [psum.tile([P, M_TILES, PIECE], F32, name=f"first{d}") for d in range(2)]
+        for d in range(2):
             for m in range(M_TILES):
-                multiply(1, m, cols, bank[:, m, :])
-            product = keep.tile([P, M_TILES, width], F32, name=f"product{i}")
-            nc.vector.tensor_tensor(product[:], bank[:], y0[:, :, cols], MULT)
-            queue = nc.scalar if i == 1 else nc.sync
-            queue.dma_start(out=out[:, cols].rearrange("(m p) v -> p m v", p=P), in_=product[:])
-            start += width
+                product(d, m, first, banks[d][:, m, :])
+        y0 = keep.tile([P, M_TILES, PIECE], F32, name="y0_first")
+        nc.scalar.copy(out=y0[:], in_=banks[0][:])
+        result = keep.tile([P, M_TILES, PIECE], F32, name="result_first")
+        nc.vector.tensor_tensor(result[:], banks[1][:], y0[:], MULT)
+        nc.sync.dma_start(out=out[:, first].rearrange("(m p) v -> p m v", p=P), in_=result[:])
+
+        for m in range(M_TILES):
+            banks = [psum.tile([P, PIECE], F32, name=f"last{d}_{m}") for d in range(2)]
+            for d in range(2):
+                product(d, m, last, banks[d][:])
+            y0 = keep.tile([P, PIECE], F32, name=f"y0_last{m}")
+            nc.scalar.copy(out=y0[:], in_=banks[0][:])
+            result = keep.tile([P, PIECE], F32, name=f"result_last{m}")
+            nc.vector.tensor_tensor(result[:], banks[1][:], y0[:], MULT)
+            queue = nc.sync if m else nc.scalar
+            queue.dma_start(out=out[m * P : (m + 1) * P, last], in_=result[:])

@@ -1,4 +1,5 @@
 import concourse.mybir as mybir
+from concourse.masks import make_identity
 
 K, T, S, V, N = 512, 4096, 1024, 512, 256
 P = 128
@@ -26,6 +27,7 @@ def tile_picked_pair_lin_mul_sub_e_kernel(tc, xT, w, offs, out):
         offsets = keep.tile([P, S // 16], U16, name="offsets")
         nc.sync.dma_start(offsets[:], offs)
 
+
         x_rows = xT.rearrange("(p j) t -> p j t", j=PACK)
         planes = []
         for j in range(PACK):
@@ -33,32 +35,28 @@ def tile_picked_pair_lin_mul_sub_e_kernel(tc, xT, w, offs, out):
             nc.sync.dma_start(out=plane[:], in_=x_rows[:, j, :])
             planes.append(plane)
 
-        w_raw = []
-        for d in range(2):
-            raw = keep.tile([P, PACK, N], F32, name=f"w_raw{d}")
-            nc.sync.dma_start(out=raw[:], in_=w[d].rearrange("(p j) n -> p j n", j=PACK))
-            w_raw.append(raw)
+        w_raw0 = keep.tile([P, PACK, N], F32, name="w_raw0")
+        nc.sync.dma_start(out=w_raw0[:], in_=w[0].rearrange("(p j) n -> p j n", j=PACK))
+        w_raw1 = keep.tile([P, PACK, N], F32, name="w_raw1")
+        nc.sync.dma_start(out=w_raw1[:], in_=w[1].rearrange("(p j) n -> p j n", j=PACK))
+        w_raw = [w_raw0, w_raw1]
 
+        w_grouped = [keep.tile([P, N, PACK], BF16, name=f"w_grouped{d}", align_bytes=64) for d in range(2)]
+        w_codes = [keep.tile([P, N], U32, name=f"w_codes{d}", align_bytes=64) for d in range(2)]
+        w_scales = [keep.tile([P, N], U8, name=f"w_scales{d}", align_bytes=64) for d in range(2)]
         x_grouped = [keep.tile([P, V, PACK], BF16, name=f"x_grouped{d}", align_bytes=64) for d in range(2)]
         x_codes = [keep.tile([P, V], U32, name=f"x_codes{d}", align_bytes=64) for d in range(2)]
         x_scales = [keep.tile([P, V], U8, name=f"x_scales{d}", align_bytes=64) for d in range(2)]
-        for j in range(PACK):
-            for d in range(2):
-                picked = planes[j][:].indirect(offsets[:, d * (V // 16) : (d + 1) * (V // 16)])
-                nc.vector.tensor_copy(x_grouped[d][:, :, j], picked)
 
-        w_codes = [keep.tile([P, N], U32, name=f"w_codes{d}", align_bytes=64) for d in range(2)]
-        w_scales = [keep.tile([P, N], U8, name=f"w_scales{d}", align_bytes=64) for d in range(2)]
-        for d in range(2):
-            w_grouped = keep.tile([P, N, PACK], BF16, name=f"w_grouped{d}", align_bytes=64)
-            nc.scalar.copy(out=w_grouped[:], in_=w_raw[d][:].rearrange("p j n -> p n j"))
+        def quantise_w(d):
+            nc.scalar.copy(out=w_grouped[d][:], in_=w_raw[d][:].rearrange("p j n -> p n j"))
             nc.vector.quantize_mx(
                 out=w_codes[d][:].bitcast(FP8X4),
                 scales=w_scales[d][:],
-                in_=w_grouped[:].rearrange("p n j -> p (n j)"),
+                in_=w_grouped[d][:].rearrange("p n j -> p (n j)"),
             )
 
-        def quantise(d, cols):
+        def quantise_x(d, cols):
             nc.vector.quantize_mx(
                 out=x_codes[d][:, cols].bitcast(FP8X4),
                 scales=x_scales[d][:, cols],
@@ -77,29 +75,33 @@ def tile_picked_pair_lin_mul_sub_e_kernel(tc, xT, w, offs, out):
                 stop=True,
             )
 
-        first = slice(0, PIECE)
-        last = slice(PIECE, 2 * PIECE)
-        for cols in (first, last):
+        for j in range(PACK):
             for d in range(2):
-                quantise(d, cols)
+                picked = planes[j][:].indirect(offsets[:, d * (V // 16) : (d + 1) * (V // 16)])
+                nc.vector.tensor_copy(x_grouped[d][:, :, j], picked)
 
-        banks = [psum.tile([P, M_TILES, PIECE], F32, name=f"first{d}") for d in range(2)]
-        for d in range(2):
+        identity = keep.tile([P, P], F32, name="identity")
+        make_identity(nc, identity[:])
+        warm = psum.tile([P, 4, P], F32, name="warm")
+        for i in range(24):
+            nc.tensor.transpose(warm[:, i % 4, :], planes[PACK - 1][:, i * P : (i + 1) * P], identity[:])
+
+        pieces = [slice(i * PIECE, (i + 1) * PIECE) for i in range(V // PIECE)]
+        y0 = [[keep.tile([P, PIECE], F32, name=f"y0_{i}_{m}") for m in range(M_TILES)] for i in range(len(pieces))]
+        quantise_w(0)
+        for i, cols in enumerate(pieces):
+            quantise_x(0, cols)
             for m in range(M_TILES):
-                product(d, m, first, banks[d][:, m, :])
-        y0 = keep.tile([P, M_TILES, PIECE], F32, name="y0_first")
-        nc.scalar.copy(out=y0[:], in_=banks[0][:])
-        result = keep.tile([P, M_TILES, PIECE], F32, name="result_first")
-        nc.vector.tensor_tensor(result[:], banks[1][:], y0[:], MULT)
-        nc.sync.dma_start(out=out[:, first].rearrange("(m p) v -> p m v", p=P), in_=result[:])
-
-        for m in range(M_TILES):
-            banks = [psum.tile([P, PIECE], F32, name=f"last{d}_{m}") for d in range(2)]
-            for d in range(2):
-                product(d, m, last, banks[d][:])
-            y0 = keep.tile([P, PIECE], F32, name=f"y0_last{m}")
-            nc.scalar.copy(out=y0[:], in_=banks[0][:])
-            result = keep.tile([P, PIECE], F32, name=f"result_last{m}")
-            nc.vector.tensor_tensor(result[:], banks[1][:], y0[:], MULT)
-            queue = nc.sync if m else nc.scalar
-            queue.dma_start(out=out[m * P : (m + 1) * P, last], in_=result[:])
+                bank = psum.tile([P, PIECE], F32, name=f"bank0_{m}")
+                product(0, m, cols, bank[:])
+                nc.scalar.copy(out=y0[i][m][:], in_=bank[:])
+        quantise_w(1)
+        for i, cols in enumerate(pieces):
+            quantise_x(1, cols)
+            for m in range(M_TILES):
+                bank = psum.tile([P, PIECE], F32, name=f"bank1_{i}_{m}")
+                product(1, m, cols, bank[:])
+                result = keep.tile([P, PIECE], F32, name=f"result{i}_{m}")
+                nc.vector.tensor_tensor(result[:], bank[:], y0[i][m][:], MULT)
+                queue = nc.sync if m else nc.scalar
+                queue.dma_start(out=out[m * P : (m + 1) * P, cols], in_=result[:])

@@ -6,6 +6,7 @@ P = 128
 PACK = 4
 M_TILES = N // P
 PIECE = 256
+PIECES = V // PIECE
 
 FLOPS = 2 * K * N * S
 
@@ -27,81 +28,107 @@ def tile_picked_pair_lin_mul_sub_e_kernel(tc, xT, w, offs, out):
         offsets = keep.tile([P, S // 16], U16, name="offsets")
         nc.sync.dma_start(offsets[:], offs)
 
-
+        w_raw = [keep.tile([P, PACK, N], F32, name=f"w_raw{d}") for d in range(2)]
+        planes = [keep.tile([P, T], F32, name=f"plane{j}") for j in range(PACK)]
         x_rows = xT.rearrange("(p j) t -> p j t", j=PACK)
-        planes = []
+        nc.sync.dma_start(out=w_raw[0][:], in_=w[0].rearrange("(p j) n -> p j n", j=PACK))
         for j in range(PACK):
-            plane = keep.tile([P, T], F32, name=f"plane{j}")
-            nc.sync.dma_start(out=plane[:], in_=x_rows[:, j, :])
-            planes.append(plane)
+            nc.sync.dma_start(out=planes[j][:], in_=x_rows[:, j, :])
+        nc.sync.dma_start(out=w_raw[1][:], in_=w[1].rearrange("(p j) n -> p j n", j=PACK))
 
-        w_raw0 = keep.tile([P, PACK, N], F32, name="w_raw0")
-        nc.sync.dma_start(out=w_raw0[:], in_=w[0].rearrange("(p j) n -> p j n", j=PACK))
-        w_raw1 = keep.tile([P, PACK, N], F32, name="w_raw1")
-        nc.sync.dma_start(out=w_raw1[:], in_=w[1].rearrange("(p j) n -> p j n", j=PACK))
-        w_raw = [w_raw0, w_raw1]
+        identity = keep.tile([P, P], F32, name="identity")
+        make_identity(nc, identity[:])
 
-        w_grouped = [keep.tile([P, N, PACK], BF16, name=f"w_grouped{d}", align_bytes=64) for d in range(2)]
-        w_codes = [keep.tile([P, N], U32, name=f"w_codes{d}", align_bytes=64) for d in range(2)]
-        w_scales = [keep.tile([P, N], U8, name=f"w_scales{d}", align_bytes=64) for d in range(2)]
-        x_grouped = [keep.tile([P, V, PACK], BF16, name=f"x_grouped{d}", align_bytes=64) for d in range(2)]
-        x_codes = [keep.tile([P, V], U32, name=f"x_codes{d}", align_bytes=64) for d in range(2)]
-        x_scales = [keep.tile([P, V], U8, name=f"x_scales{d}", align_bytes=64) for d in range(2)]
+        w_grouped = [[keep.tile([P, P, PACK], BF16, name=f"w_grouped{d}_{m}", align_bytes=64) for m in range(M_TILES)] for d in range(2)]
+        w_codes = [[keep.tile([P, P], U32, name=f"w_codes{d}_{m}", align_bytes=64) for m in range(M_TILES)] for d in range(2)]
+        w_scales = [[keep.tile([P, P], U8, name=f"w_scales{d}_{m}", align_bytes=64) for m in range(M_TILES)] for d in range(2)]
+        gathered = [[keep.tile([P, 2, V], F32, name=f"gathered{d}_{u}") for u in range(2)] for d in range(2)]
+        x_grouped = [[keep.tile([P, PIECE, PACK], BF16, name=f"x_grouped{d}_{i}", align_bytes=64) for i in range(PIECES)] for d in range(2)]
+        x_codes = [[keep.tile([P, PIECE], U32, name=f"x_codes{d}_{i}", align_bytes=64) for i in range(PIECES)] for d in range(2)]
+        x_scales = [[keep.tile([P, PIECE], U8, name=f"x_scales{d}_{i}", align_bytes=64) for i in range(PIECES)] for d in range(2)]
+        pieces = [slice(i * PIECE, (i + 1) * PIECE) for i in range(PIECES)]
 
-        def quantise_w(d):
-            nc.scalar.copy(out=w_grouped[d][:], in_=w_raw[d][:].rearrange("p j n -> p n j"))
-            nc.vector.quantize_mx(
-                out=w_codes[d][:].bitcast(FP8X4),
-                scales=w_scales[d][:],
-                in_=w_grouped[d][:].rearrange("p n j -> p (n j)"),
+        def interleave_w(d, m):
+            nc.scalar.copy(
+                out=w_grouped[d][m][:],
+                in_=w_raw[d][:, :, m * P : (m + 1) * P].rearrange("p j n -> p n j"),
             )
 
-        def quantise_x(d, cols):
+        def quantise_w(d, m):
             nc.vector.quantize_mx(
-                out=x_codes[d][:, cols].bitcast(FP8X4),
-                scales=x_scales[d][:, cols],
-                in_=x_grouped[d][:, cols, :].rearrange("p v j -> p (v j)"),
+                out=w_codes[d][m][:].bitcast(FP8X4),
+                scales=w_scales[d][m][:],
+                in_=w_grouped[d][m][:].rearrange("p n j -> p (n j)"),
             )
 
-        def product(d, m, cols, acc):
-            m_cols = slice(m * P, (m + 1) * P)
+        def gather(j, d):
+            picked = planes[j][:].indirect(offsets[:, d * (V // 16) : (d + 1) * (V // 16)])
+            nc.vector.tensor_copy(gathered[d][j // 2][:, j % 2, :], picked)
+
+        def interleave_x(copy, d, i, u):
+            copy(
+                out=x_grouped[d][i][:, :, 2 * u : 2 * u + 2],
+                in_=gathered[d][u][:, :, pieces[i]].rearrange("p e v -> p v e"),
+            )
+
+        def quantise_x(d, i):
+            nc.vector.quantize_mx(
+                out=x_codes[d][i][:].bitcast(FP8X4),
+                scales=x_scales[d][i][:],
+                in_=x_grouped[d][i][:].rearrange("p v j -> p (v j)"),
+            )
+
+        def product(d, i, m, acc):
             nc.tensor.matmul_mx(
                 out=acc,
-                lhsT=w_codes[d][:, m_cols].bitcast(FP8X4),
-                lhsT_scale=w_scales[d][:, m_cols],
-                rhs=x_codes[d][:, cols].bitcast(FP8X4),
-                rhs_scale=x_scales[d][:, cols],
+                lhsT=w_codes[d][m][:].bitcast(FP8X4),
+                lhsT_scale=w_scales[d][m][:],
+                rhs=x_codes[d][i][:].bitcast(FP8X4),
+                rhs_scale=x_scales[d][i][:],
                 start=True,
                 stop=True,
             )
 
+        for m in range(M_TILES):
+            interleave_w(0, m)
+        for m in range(M_TILES):
+            quantise_w(0, m)
         for j in range(PACK):
             for d in range(2):
-                picked = planes[j][:].indirect(offsets[:, d * (V // 16) : (d + 1) * (V // 16)])
-                nc.vector.tensor_copy(x_grouped[d][:, :, j], picked)
+                gather(j, d)
+            if j == 1:
+                for d in range(2):
+                    for i in range(PIECES):
+                        interleave_x(nc.scalar.copy, d, i, 0)
 
-        identity = keep.tile([P, P], F32, name="identity")
-        make_identity(nc, identity[:])
-        warm = psum.tile([P, 4, P], F32, name="warm")
-        for i in range(24):
+        warm = psum.tile([P, 4, P], F32, name="warm", tag="spare")
+        for i in range(12):
             nc.tensor.transpose(warm[:, i % 4, :], planes[PACK - 1][:, i * P : (i + 1) * P], identity[:])
 
-        pieces = [slice(i * PIECE, (i + 1) * PIECE) for i in range(V // PIECE)]
-        y0 = [[keep.tile([P, PIECE], F32, name=f"y0_{i}_{m}") for m in range(M_TILES)] for i in range(len(pieces))]
-        quantise_w(0)
-        for i, cols in enumerate(pieces):
-            quantise_x(0, cols)
+        for i in range(PIECES):
+            interleave_x(nc.scalar.copy, 0, i, 1)
+            interleave_x(nc.vector.tensor_copy, 1, i, 1)
+        for m in range(M_TILES):
+            interleave_w(1, m)
+
+        y0 = {}
+        for i in range(PIECES):
+            quantise_x(0, i)
             for m in range(M_TILES):
-                bank = psum.tile([P, PIECE], F32, name=f"bank0_{m}")
-                product(0, m, cols, bank[:])
-                nc.scalar.copy(out=y0[i][m][:], in_=bank[:])
-        quantise_w(1)
-        for i, cols in enumerate(pieces):
-            quantise_x(1, cols)
-            for m in range(M_TILES):
-                bank = psum.tile([P, PIECE], F32, name=f"bank1_{i}_{m}")
-                product(1, m, cols, bank[:])
+                bank = psum.tile([P, PIECE], F32, name=f"bank0_{i}_{m}")
+                product(0, i, m, bank[:])
+                y0[i, m] = keep.tile([P, PIECE], F32, name=f"y0_{i}_{m}")
+                nc.scalar.copy(out=y0[i, m][:], in_=bank[:])
+        quantise_x(1, 0)
+        quantise_w(1, 0)
+        quantise_x(1, 1)
+        quantise_w(1, 1)
+        for m in range(M_TILES):
+            for i in range(PIECES):
+                final = (m, i) == (M_TILES - 1, PIECES - 1)
+                bank = psum.tile([P, PIECE], F32, name=f"bank1_{i}_{m}", tag="spare" if final else f"bank1_{i}_{m}")
+                product(1, i, m, bank[:])
                 result = keep.tile([P, PIECE], F32, name=f"result{i}_{m}")
-                nc.vector.tensor_tensor(result[:], bank[:], y0[i][m][:], MULT)
-                queue = nc.sync if m else nc.scalar
-                queue.dma_start(out=out[m * P : (m + 1) * P, cols], in_=result[:])
+                nc.vector.tensor_tensor(result[:], bank[:], y0[i, m][:], MULT)
+                queue = nc.sync if i else nc.scalar
+                queue.dma_start(out=out[m * P : (m + 1) * P, pieces[i]], in_=result[:])

import concourse.mybir as mybir
from concourse.masks import make_identity

K, T, S, V, N = 512, 4096, 1024, 512, 256
P = 128
PACK = 4
M_TILES = N // P
PIECE = 256
PIECES = V // PIECE

FLOPS = 2 * K * N * S

F32 = mybir.dt.float32
BF16 = mybir.dt.bfloat16
U32 = mybir.dt.uint32
U16 = mybir.dt.uint16
U8 = mybir.dt.uint8
FP8X4 = mybir.dt.float8_e4m3fn_x4
MULT = mybir.AluOpType.mult


def tile_picked_pair_lin_mul_sub_e_kernel(tc, xT, w, offs, out):
    nc = tc.nc
    with (
        tc.tile_pool(name="keep", bufs=1) as keep,
        tc.psum_pool(name="psum", bufs=1) as psum,
    ):
        offsets = keep.tile([P, S // 16], U16, name="offsets")
        nc.sync.dma_start(offsets[:], offs)

        w_raw = [keep.tile([P, PACK, N], F32, name=f"w_raw{d}") for d in range(2)]
        planes = [keep.tile([P, T], F32, name=f"plane{j}") for j in range(PACK)]
        x_rows = xT.rearrange("(p j) t -> p j t", j=PACK)
        nc.sync.dma_start(out=w_raw[0][:], in_=w[0].rearrange("(p j) n -> p j n", j=PACK))
        for j in range(PACK):
            nc.sync.dma_start(out=planes[j][:], in_=x_rows[:, j, :])
        nc.sync.dma_start(out=w_raw[1][:], in_=w[1].rearrange("(p j) n -> p j n", j=PACK))

        identity = keep.tile([P, P], F32, name="identity")
        make_identity(nc, identity[:])

        w_grouped = [[keep.tile([P, P, PACK], BF16, name=f"w_grouped{d}_{m}", align_bytes=64) for m in range(M_TILES)] for d in range(2)]
        w_codes = [[keep.tile([P, P], U32, name=f"w_codes{d}_{m}", align_bytes=64) for m in range(M_TILES)] for d in range(2)]
        w_scales = [[keep.tile([P, P], U8, name=f"w_scales{d}_{m}", align_bytes=64) for m in range(M_TILES)] for d in range(2)]
        gathered = [[keep.tile([P, 2, V], F32, name=f"gathered{d}_{u}") for u in range(2)] for d in range(2)]
        x_grouped = [[keep.tile([P, PIECE, PACK], BF16, name=f"x_grouped{d}_{i}", align_bytes=64) for i in range(PIECES)] for d in range(2)]
        x_codes = [[keep.tile([P, PIECE], U32, name=f"x_codes{d}_{i}", align_bytes=64) for i in range(PIECES)] for d in range(2)]
        x_scales = [[keep.tile([P, PIECE], U8, name=f"x_scales{d}_{i}", align_bytes=64) for i in range(PIECES)] for d in range(2)]
        pieces = [slice(i * PIECE, (i + 1) * PIECE) for i in range(PIECES)]

        def interleave_w(d, m):
            nc.scalar.copy(
                out=w_grouped[d][m][:],
                in_=w_raw[d][:, :, m * P : (m + 1) * P].rearrange("p j n -> p n j"),
            )

        def quantise_w(d, m):
            nc.vector.quantize_mx(
                out=w_codes[d][m][:].bitcast(FP8X4),
                scales=w_scales[d][m][:],
                in_=w_grouped[d][m][:].rearrange("p n j -> p (n j)"),
            )

        def gather(j, d):
            picked = planes[j][:].indirect(offsets[:, d * (V // 16) : (d + 1) * (V // 16)])
            nc.vector.tensor_copy(gathered[d][j // 2][:, j % 2, :], picked)

        def interleave_x(copy, d, i, u):
            copy(
                out=x_grouped[d][i][:, :, 2 * u : 2 * u + 2],
                in_=gathered[d][u][:, :, pieces[i]].rearrange("p e v -> p v e"),
            )

        def quantise_x(d, i):
            nc.vector.quantize_mx(
                out=x_codes[d][i][:].bitcast(FP8X4),
                scales=x_scales[d][i][:],
                in_=x_grouped[d][i][:].rearrange("p v j -> p (v j)"),
            )

        def product(d, i, m, acc):
            nc.tensor.matmul_mx(
                out=acc,
                lhsT=w_codes[d][m][:].bitcast(FP8X4),
                lhsT_scale=w_scales[d][m][:],
                rhs=x_codes[d][i][:].bitcast(FP8X4),
                rhs_scale=x_scales[d][i][:],
                start=True,
                stop=True,
            )

        for m in range(M_TILES):
            interleave_w(0, m)
        for m in range(M_TILES):
            quantise_w(0, m)
        for j in range(PACK):
            for d in range(2):
                gather(j, d)
            if j == 1:
                for d in range(2):
                    for i in range(PIECES):
                        interleave_x(nc.scalar.copy, d, i, 0)

        warm = psum.tile([P, 4, P], F32, name="warm", tag="spare")
        for i in range(12):
            nc.tensor.transpose(warm[:, i % 4, :], planes[PACK - 1][:, i * P : (i + 1) * P], identity[:])

        for i in range(PIECES):
            interleave_x(nc.scalar.copy, 0, i, 1)
            interleave_x(nc.vector.tensor_copy, 1, i, 1)
        for m in range(M_TILES):
            interleave_w(1, m)

        y0 = {}
        for i in range(PIECES):
            quantise_x(0, i)
            for m in range(M_TILES):
                bank = psum.tile([P, PIECE], F32, name=f"bank0_{i}_{m}")
                product(0, i, m, bank[:])
                y0[i, m] = keep.tile([P, PIECE], F32, name=f"y0_{i}_{m}")
                nc.scalar.copy(out=y0[i, m][:], in_=bank[:])
        quantise_x(1, 0)
        quantise_w(1, 0)
        quantise_x(1, 1)
        quantise_w(1, 1)
        for m in range(M_TILES):
            for i in range(PIECES):
                final = (m, i) == (M_TILES - 1, PIECES - 1)
                bank = psum.tile([P, PIECE], F32, name=f"bank1_{i}_{m}", tag="spare" if final else f"bank1_{i}_{m}")
                product(1, i, m, bank[:])
                result = keep.tile([P, PIECE], F32, name=f"result{i}_{m}")
                nc.vector.tensor_tensor(result[:], bank[:], y0[i, m][:], MULT)
                queue = nc.sync if i else nc.scalar
                queue.dma_start(out=out[m * P : (m + 1) * P, pieces[i]], in_=result[:])
